import numpy as np, ml_dtypes
CORES = [2,3,42,43,82,83,122,123]
N = 8
import mx_ref
BF = ml_dtypes.bfloat16
def entries(a):
    return np.ascontiguousarray(a.T).reshape(-1)
def table(e):
    return np.ascontiguousarray(np.reshape(e, (-1, 16)).T).astype(np.int32)
def cols(t, e):
    v = np.concatenate([t.reshape(128, -1, 4), np.zeros((128, 1, 4), BF)], axis=1)
    return np.ascontiguousarray(v[:, e]).reshape(128, -1)
def f(rng, *shape):
    return mx_ref.flush((rng.standard_normal(shape, dtype=np.float32) * np.exp2(rng.integers(-2, 3, shape[:-1] + (1,)))).astype(BF))
def wide(rng, *shape, cols=0):
    v = rng.standard_normal(shape, dtype=np.float32) * np.exp2(rng.integers(-12, 13, shape)).astype(np.float32)
    if cols: v *= np.repeat(np.exp2(rng.integers(-cols, cols + 1, shape[:-2] + (1, shape[-1] // 4))) * (rng.random(shape[:-2] + (1, shape[-1] // 4)) > 0.0625), 4, axis=-1).astype(np.float32)
    return mx_ref.flush(v.astype(BF))
T, NA, S, CAPP = 1024, 512, 512, 96
def lists(rng, most=0, inorder=False, big=None):
    c, m = [], []
    for r in range(N):
        n = np.zeros(N, int)
        n[rng.permutation(N)[:most]] = CAPP
        while n.sum() < S:
            q = rng.integers(0, N)
            if n[q] < CAPP: n[q] += 1
        used = np.concatenate([q * CAPP + rng.permutation(CAPP)[:n[q]] for q in range(N)])
        slots = np.full(N * CAPP, -1); slots[used] = rng.integers(0, T, S)
        o = np.sort(used) if inorder else rng.permutation(used)
        if big is not None:
            for i in range(S // 32):
                k = o[32 * i + rng.integers(0, 32)]; slots[k] = rng.choice(big[k // CAPP])
        c.append(table(slots)); m.append(table(o))
    return {"want": np.stack(c), "slot": np.stack(m)}
def setup_inputs(rng):
    return {"v": f(rng, N, 128, 4 * T), "a": f(rng, N, 128, 4 * NA), **lists(rng)}
def setup_inputs_full(rng):
    return {**setup_inputs(rng), **lists(rng, most=S // CAPP)}
def setup_inputs_sorted(rng):
    return {**setup_inputs(rng), **lists(rng, inorder=True)}
def setup_inputs_giant(rng):
    d = setup_inputs(rng); big = [rng.permutation(T)[:T // 32] for q in range(N)]
    x = d["v"].reshape(N, 128, T, 4)
    for q in range(N): x[q][:, big[q]] = (x[q][:, big[q]].astype(np.float32) * np.float32(2.0 ** 20)).astype(BF)
    d["v"] = x.reshape(N, 128, 4 * T)
    return {**d, **lists(rng, big=big)}
def setup_inputs_spread(rng):
    d = setup_inputs(rng); d["v"] = wide(rng, N, 128, 4 * T); d["a"] = wide(rng, N, 128, 4 * NA); return d
def check_inputs(d):
    b = []
    for r in range(N):
        c, m = entries(d["want"][r]), entries(d["slot"][r])
        if c.min() < -1 or c.max() >= T or (c >= 0).sum() != S: b.append("want")
        if m.min() < 0 or m.max() >= N * CAPP or len(set(m.tolist())) != S or (c[np.clip(m, 0, N * CAPP - 1)] < 0).any(): b.append("slot")
    return b
def ones(b):
    e = np.zeros((128, 128, 4), np.float32); e[np.arange(128), np.arange(128), b] = 1
    return e.reshape(128, 512).astype(BF)
def decode(q):
    return np.stack([mx_ref.matmul(mx_ref.quantize(ones(b)), q) for b in range(4)], axis=1).reshape(512, -1)
def reference(v, a, want, slot, own=None):
    h = np.zeros((N, 128, 2048), BF); y = np.zeros((N, 128, 4 * NA), np.float32)
    for r in range(N):
        c = entries(want[r])
        arrived = np.concatenate([decode(mx_ref.quantize(cols(v[q], c[q * CAPP:(q + 1) * CAPP]))) for q in range(N)], axis=1)
        H = arrived[:, entries(slot[r])].T
        h[r] = H.reshape(128, 4, 512).transpose(0, 2, 1).reshape(128, 2048).astype(BF)
    for r in range(N):
        t = h[r] if own is None else np.asarray(own["h"][r])
        for o in range(4):
            y[r][:, NA * o:NA * o + NA] = mx_ref.matmul(mx_ref.quantize(np.ascontiguousarray(t[:, 512 * o:512 * o + 512])), mx_ref.quantize(a[r]))
    return {"y": y, "h": h}

@@ -1,0 +1,223 @@
+from concourse.bass import DstId, RemoteDMATransfer
+from concourse.mybir import dt, AluOpType, ActivationFunctionType
+
+N, CAPP, HALF = 8, 96, 4
+NA, NB = (HALF - 1) * CAPP, HALF * CAPP
+L = CAPP // 16
+E4 = "float8_e4m3fn_x4"
+
+SCRATCH = {
+    "wraw": ("sbuf", [128, N * L], "int32"), "wl": ("sbuf", [128, N * L], "uint16"),
+    "sraw": ("sbuf", [128, 32], "int32"), "so": ("sbuf", [128, 32], "uint16"),
+    "la": ("sbuf", [128, (HALF - 1) * L], "uint16"), "lb": ("sbuf", [128, HALF * L], "uint16"),
+    "vt": ("sbuf", [128, 4096], "bfloat16"), "at": ("sbuf", [128, 2048], "bfloat16"),
+    "town": ("sbuf", [128, 512], "bfloat16"), "ta": ("sbuf", [128, 4 * NA], "bfloat16"), "tb": ("sbuf", [128, 4 * NB], "bfloat16"),
+    "qo": ("sbuf", [128, 128], E4), "xo": ("sbuf", [128, 128], "uint8"),
+    "qa": ("sbuf", [128, NA], E4), "xa": ("sbuf", [128, NA], "uint8"),
+    "qb": ("sbuf", [128, NB], E4), "xb": ("sbuf", [128, NB], "uint8"),
+    "ra": ("sbuf", [128, NA], E4), "rxa": ("sbuf", [128, NA], "uint8"),
+    "rb": ("sbuf", [128, NB], E4), "rxb": ("sbuf", [128, NB], "uint8"),
+    "qm": ("sbuf", [128, 512], E4), "xm": ("sbuf", [128, 512], "uint8"),
+    "kk": ("sbuf", [128, 512], "bfloat16"), "kc": ("sbuf", [128, 4], "float32"), "et": ("sbuf", [128, 2048], "bfloat16"),
+    "qe": ("sbuf", [128, 512], E4), "xe": ("sbuf", [128, 512], "uint8"),
+    "kd": ("sbuf", [128, 128], "float32"), "idn": ("sbuf", [128, 128], "float32"),
+    "win": ("sbuf", [128, 4 * N * CAPP], "bfloat16"), "gt": ("sbuf", [128, 2048], "float32"),
+    "ht": ("sbuf", [128, 2048], "bfloat16"), "qh": ("sbuf", [128, 512], E4), "xh": ("sbuf", [128, 512], "uint8"),
+    "yt": ("sbuf", [128, 2048], "float32"),
+    "p0": ("psum", [128, 2048], "float32"), "p1": ("psum", [128, 2048], "float32"),
+}
+SEMAPHORES = (["sw", "ss", "sv", "sa", "swl", "sso", "szo", "sk", "se", "sqe", "sdn", "sqm", "sla", "slb", "ara", "arb", "loc",
+               "gov", "gos", "gav", "gas", "gbv", "gbs", "sqo", "sqa", "sqb", "sh", "sy"]
+              + ["%s%d" % (n, b) for n in ("mo", "ma", "mb", "co", "ca", "cb", "gg", "tt", "hh", "hq", "ym", "yc") for b in range(4)])
+
+
+def rank_program(g, core, T, topo):
+    r = T.rank_of(core)
+    if r is None:
+        return
+    S = T.sem
+    v, s, te, sy = g.vector, g.scalar, g.tensor, g.sync
+    Copy = ActivationFunctionType.Copy
+    cores = T.cores
+    mine = [q for q in range(N) if q // HALF == r // HALF and q != r]
+    other = [q for q in range(N) if q // HALF != r // HALF]
+
+    near = [q for q in mine if topo.chip(cores[q]) == topo.chip(core)]
+    far = [q for q in mine if q not in near]
+    off = topo.engines(core, cores[other[0]])
+    on = [e for e in topo.engines(core, cores[near[0]]) if e not in off]
+
+    def msk(es):
+        return sum(1 << e for e in es)
+
+    eng = {q: on[4 * i:4 * i + 4] for i, q in enumerate(near)}
+    w = len(off) // len(far)
+    eng.update({q: off[w * i:w * i + w] for i, q in enumerate(far)})
+    w = len(off) // len(other)
+    eng.update({q: off[w * i:w * i + w] for i, q in enumerate(other)})
+    engs = lambda src, dst: 4 if topo.chip(cores[src]) == topo.chip(cores[dst]) else len(off) // (2 if src // HALF == dst // HALF else 4)
+    place = lambda src, dst: [q for q in range(N) if q // HALF == src // HALF and q != dst].index(src)
+
+    def send(dsts, src, dst, sem):
+        tr = []
+        for i, q in enumerate(dsts):
+            rid, pid, _ = topo.addr(cores[q])
+            tr.append(RemoteDMATransfer(dst_ids=[DstId(rid=rid, pnc=pid)], dma_engine_mask=msk(eng[q]), remote_sem=sem,
+                                        src=src(i, q), dst=dst(place(r, q)), alu_op=0))
+        g.remote_dma_fused(tr, local_sem=S.loc)
+        return sum(len(eng[q]) for q in dsts)
+
+    inA = sum(engs(q, r) for q in mine)
+    inB = sum(engs(q, r) for q in other)
+
+    for k in range(8):
+        (sy if k % 2 == 0 else s).dma_start(out=T.wraw[16 * k:16 * k + 16, :], in_=T.want[:]).then_inc(S.sw, 16)
+    sy.dma_start(out=T.vt[:], in_=T.v[:]).then_inc(S.sv, 16)
+    for k in range(8):
+        sy.dma_start(out=T.sraw[16 * k:16 * k + 16, :], in_=T.slot[:]).then_inc(S.ss, 16)
+    sy.dma_start(out=T.at[:], in_=T.a[:]).then_inc(S.sa, 16)
+
+    g.iota(T.kk[:], [[1, 128], [-1, 4]], 0, 0, allow_small_or_imprecise_dtypes=True).then_inc(S.sk, 1)
+    g.iota(T.kc[:], [[-128, 4]], 0, 4, allow_small_or_imprecise_dtypes=True).then_inc(S.sk, 1)
+    g.iota(T.kd[:], [[1, 128]], 0, -1, allow_small_or_imprecise_dtypes=True).then_inc(S.sk, 1)
+    gone = 0
+    g.wait_ge(S.swl, 1)
+    gone += send(mine, lambda i, q: T.wl[:, L * q:L * q + L], lambda k: T.la[:, L * k:L * k + L], S.sla)
+    gone += send(other, lambda i, q: T.wl[:, L * q:L * q + L], lambda k: T.lb[:, L * k:L * k + L], S.slb)
+    for sem, dsts, qs, xs, qd, xd, arr in ((S.sqa, mine, T.qa, T.xa, T.ra, T.rxa, S.ara), (S.sqb, other, T.qb, T.xb, T.rb, T.rxb, S.arb)):
+        g.wait_ge(sem, 1)
+        gone += send(dsts, lambda i, q: qs[:, CAPP * i:CAPP * i + CAPP].bitcast(dt.uint8),
+                     lambda k: qd[:, CAPP * k:CAPP * k + CAPP].bitcast(dt.uint8), arr)
+        gone += send(dsts, lambda i, q: xs[:, CAPP * i:CAPP * i + CAPP], lambda k: xd[:, CAPP * k:CAPP * k + CAPP], arr)
+    g.wait_ge(S.loc, gone)
+
+    v.wait_ge(S.sw, 128)
+    v.tensor_scalar(T.wl[:], T.wraw[:], 0.0, 4.0, AluOpType.max, AluOpType.mult).then_inc(S.swl, 1)
+    v.memset(T.town[:, 4 * CAPP:512], 0.0).then_inc(S.szo, 1)
+    v.wait_ge(S.sk, 3)
+    for b in range(4):
+        v.tensor_scalar(T.et[:, 512 * b:512 * b + 512], T.kk[:], T.kc[:, b:b + 1], None, AluOpType.is_equal).then_inc(S.se, 1)
+    v.tensor_scalar(T.idn[:], T.kd[:], 0.0, None, AluOpType.is_equal).then_inc(S.sdn, 1)
+    v.wait_ge(S.se, 4)
+    v.quantize_mx(T.qe[:], T.xe[:], T.et[:]).then_inc(S.sqe, 1)
+    v.wait_ge(S.ss, 128)
+    v.tensor_copy(T.so[:], T.sraw[:]).then_inc(S.sso, 1)
+
+    v.wait_ge(S.sv, 16)
+    s.wait_ge(S.sv, 16)
+
+    def gather(wait, tile, n, offs, sv_, ss_):
+        v.wait_ge(*wait)
+        s.wait_ge(*wait)
+        for t in range(4):
+            out, in_ = tile[:, t:4 * n:4], T.vt[:, t:4096].indirect(offs)
+            if t < 2:
+                v.tensor_copy(out, in_).then_inc(sv_, 1)
+            else:
+                s.activation(out, in_, Copy).then_inc(ss_, 1)
+        v.wait_ge(sv_, 2)
+        v.wait_ge(ss_, 2)
+
+    gather((S.sla, inA), T.ta, NA, T.la[:], S.gav, S.gas)
+    v.quantize_mx(T.qa[:], T.xa[:], T.ta[:]).then_inc(S.sqa, 1)
+    gather((S.slb, inB), T.tb, NB, T.lb[:], S.gbv, S.gbs)
+    v.quantize_mx(T.qb[:], T.xb[:], T.tb[:]).then_inc(S.sqb, 1)
+    gather((S.swl, 1), T.town, CAPP, T.wl[:, L * r:L * r + L], S.gov, S.gos)
+    v.wait_ge(S.szo, 1)
+    v.quantize_mx(T.qo[:], T.xo[:], T.town[:]).then_inc(S.sqo, 1)
+    v.wait_ge(S.sa, 16)
+    v.quantize_mx(T.qm[:], T.xm[:], T.at[:]).then_inc(S.sqm, 1)
+
+    te.wait_ge(S.sqe, 1)
+    te.wait_ge(S.sqo, 1)
+
+    def unpack(ps, n, q, x, name):
+        for b in range(4):
+            if name == "mb":
+                te.wait_ge(S["co%d" % b], 1)
+            te.matmul_mx(ps[:, 512 * b:512 * b + n], T.qe[:, 128 * b:128 * b + 128], T.xe[:, 128 * b:128 * b + 128],
+                         q[:, 0:n], x[:, 0:n], True, True).then_inc(S["%s%d" % (name, b)], 1)
+
+    unpack(T.p0, 128, T.qo, T.xo, "mo")
+    te.wait_ge(S.ara, 2 * inA)
+    unpack(T.p1, NA, T.ra, T.rxa, "ma")
+    te.wait_ge(S.arb, 2 * inB)
+    unpack(T.p0, NB, T.rb, T.rxb, "mb")
+
+    def copy(b, out, in_, sem):
+        if b % 2 == 0:
+            v.tensor_copy(out, in_).then_inc(sem, 1)
+        else:
+            s.activation(out, in_, Copy).then_inc(sem, 1)
+
+    def queue(b):
+        return v if b % 2 == 0 else s
+
+    def runs(ranks):
+        res = []
+        for k, q in enumerate(ranks):
+            if res and res[-1][1] + res[-1][2] == q:
+                res[-1][2] += 1
+            else:
+                res.append([k, q, 1])
+        return res
+
+    def store(name, m, ps, ranks, bs):
+        for b in bs:
+            queue(b).wait_ge(S["%s%d" % (m, b)], 1)
+            for k, q, n in runs(ranks):
+                copy(b, T.win[:, N * CAPP * b + CAPP * q:N * CAPP * b + CAPP * (q + n)],
+                     ps[:, 512 * b + CAPP * k:512 * b + CAPP * (k + n)], S["%s%d" % (name, b)])
+
+    store("co", "mo", T.p0, [r], range(4))
+    store("ca", "ma", T.p1, mine, range(4))
+    for pair in ((0, 1), (2, 3)):
+        store("cb", "mb", T.p0, other, pair)
+        for b in pair:
+            qu = queue(b)
+            qu.wait_ge(S.sso, 1)
+            qu.wait_ge(S["co%d" % b], 1)
+            qu.wait_ge(S["ca%d" % b], len(runs(mine)))
+            qu.wait_ge(S["cb%d" % b], 1)
+            copy(b, T.gt[:, 512 * b:512 * b + 512], T.win[:, N * CAPP * b:N * CAPP * (b + 1)].indirect(T.so[:]), S["gg%d" % b])
+
+    def turn(b):
+        te.wait_ge(S["gg%d" % b], 1)
+        for t in range(4):
+            te.transpose(T.p1[:, 512 * b + t:512 * b + 512:4], T.gt[:, 512 * b + t:512 * b + 512:4], T.idn[:]).then_inc(S["tt%d" % b], 1)
+
+    def product(b):
+        te.wait_ge(S["hq%d" % b], 1)
+        te.matmul_mx(T.p0[:, 512 * b:512 * b + 512], T.qh[:, 128 * b:128 * b + 128], T.xh[:, 128 * b:128 * b + 128],
+                     T.qm[:], T.xm[:], True, True).then_inc(S["ym%d" % b], 1)
+
+    te.wait_ge(S.sdn, 1)
+    te.wait_ge(S.sqm, 1)
+    turn(0)
+    turn(1)
+    product(0)
+    turn(2)
+    product(1)
+    turn(3)
+    product(2)
+    product(3)
+
+    for b in range(4):
+        c = slice(512 * b, 512 * b + 512)
+        v.wait_ge(S["tt%d" % b], 4)
+        v.tensor_copy(T.ht[:, c], T.p1[:, c]).then_inc(S["hh%d" % b], 1)
+        v.wait_ge(S["hh%d" % b], 1)
+        v.quantize_mx(T.qh[:, 128 * b:128 * b + 128], T.xh[:, 128 * b:128 * b + 128], T.ht[:, c]).then_inc(S["hq%d" % b], 1)
+        s.wait_ge(S["ym%d" % b], 1)
+        s.activation(T.yt[:, c], T.p0[:, c], Copy).then_inc(S["yc%d" % b], 1)
+
+    for what, b in (("h", 0), ("h", 1), ("y", 0), ("h", 2), ("y", 1), ("h", 3), ("y", 2), ("y", 3)):
+        c = slice(512 * b, 512 * b + 512)
+        if what == "h":
+            sy.wait_ge(S["hh%d" % b], 1)
+            sy.dma_start(out=T.h[:, c], in_=T.ht[:, c]).then_inc(S.sh, 16)
+        else:
+            sy.wait_ge(S["yc%d" % b], 1)
+            sy.dma_start(out=T.y[:, c], in_=T.yt[:, c]).then_inc(S.sy, 16)
+    sy.wait_ge(S.sh, 64)
+    sy.wait_ge(S.sy, 64)

@@ -1,34 +1,40 @@
 from concourse.bass import DstId, RemoteDMATransfer
 from concourse.mybir import dt, AluOpType, ActivationFunctionType
 
-N, CAPP, HALF = 8, 96, 4
-NA, NB = (HALF - 1) * CAPP, HALF * CAPP
+N, CAPP = 8, 96
 L = CAPP // 16
+P2 = 2 * CAPP
 E4 = "float8_e4m3fn_x4"
 
 SCRATCH = {
     "wraw": ("sbuf", [128, N * L], "int32"), "wl": ("sbuf", [128, N * L], "uint16"),
-    "sraw": ("sbuf", [128, 32], "int32"), "so": ("sbuf", [128, 32], "uint16"),
-    "la": ("sbuf", [128, (HALF - 1) * L], "uint16"), "lb": ("sbuf", [128, HALF * L], "uint16"),
+    "sraw": ("sbuf", [128, 32], "int32"), "sn": ("sbuf", [128, 32], "uint16"), "so": ("sbuf", [128, 32], "uint16"),
+    "sx": ("sbuf", [128, 64], "float32"), "st": ("sbuf", [128, 64], "float32"),
+    "l0": ("sbuf", [128, 2 * L], "uint16"), "l1": ("sbuf", [128, 3 * L], "uint16"), "l2": ("sbuf", [128, 2 * L], "uint16"),
     "vt": ("sbuf", [128, 4096], "bfloat16"), "at": ("sbuf", [128, 2048], "bfloat16"),
-    "town": ("sbuf", [128, 512], "bfloat16"), "ta": ("sbuf", [128, 4 * NA], "bfloat16"), "tb": ("sbuf", [128, 4 * NB], "bfloat16"),
-    "qo": ("sbuf", [128, 128], E4), "xo": ("sbuf", [128, 128], "uint8"),
-    "qa": ("sbuf", [128, NA], E4), "xa": ("sbuf", [128, NA], "uint8"),
-    "qb": ("sbuf", [128, NB], E4), "xb": ("sbuf", [128, NB], "uint8"),
-    "ra": ("sbuf", [128, NA], E4), "rxa": ("sbuf", [128, NA], "uint8"),
-    "rb": ("sbuf", [128, NB], E4), "rxb": ("sbuf", [128, NB], "uint8"),
+    "t0": ("sbuf", [128, 4 * P2], "bfloat16"), "t1": ("sbuf", [128, 4 * (P2 + CAPP)], "bfloat16"), "t2": ("sbuf", [128, 4 * P2], "bfloat16"),
+    "q0": ("sbuf", [128, P2], E4), "x0": ("sbuf", [128, P2], "uint8"),
+    "q1": ("sbuf", [128, P2 + CAPP], E4), "x1": ("sbuf", [128, P2 + CAPP], "uint8"),
+    "q2": ("sbuf", [128, P2], E4), "x2": ("sbuf", [128, P2], "uint8"),
+    "town": ("sbuf", [128, 512], "bfloat16"),
+    "r0": ("sbuf", [128, P2], E4), "rx0": ("sbuf", [128, P2], "uint8"),
+    "r1": ("sbuf", [128, P2], E4), "rx1": ("sbuf", [128, P2], "uint8"),
+    "r2": ("sbuf", [128, P2], E4), "rx2": ("sbuf", [128, P2], "uint8"),
+    "rn": ("sbuf", [128, 224], E4), "rxn": ("sbuf", [128, 224], "uint8"),
     "qm": ("sbuf", [128, 512], E4), "xm": ("sbuf", [128, 512], "uint8"),
-    "kk": ("sbuf", [128, 512], "bfloat16"), "kc": ("sbuf", [128, 4], "float32"), "et": ("sbuf", [128, 2048], "bfloat16"),
-    "qe": ("sbuf", [128, 512], E4), "xe": ("sbuf", [128, 512], "uint8"),
+    "kk": ("sbuf", [128, 512], "bfloat16"), "kc": ("sbuf", [128, 2], "float32"), "kb": ("sbuf", [128, 8], "float32"),
     "kd": ("sbuf", [128, 128], "float32"), "idn": ("sbuf", [128, 128], "float32"),
-    "win": ("sbuf", [128, 4 * N * CAPP], "bfloat16"), "gt": ("sbuf", [128, 2048], "float32"),
+    "et": ("sbuf", [128, 2048], "bfloat16"), "qe": ("sbuf", [128, 512], E4), "xe": ("sbuf", [128, 512], "uint8"),
+    "win": ("sbuf", [128, 4 * N * CAPP], "bfloat16"),
+    "gf": ("sbuf", [128, 1024], "float32"), "gb": ("sbuf", [128, 1024], "bfloat16"), "tr": ("sbuf", [128, 1024], "bfloat16"),
     "ht": ("sbuf", [128, 2048], "bfloat16"), "qh": ("sbuf", [128, 512], E4), "xh": ("sbuf", [128, 512], "uint8"),
     "yt": ("sbuf", [128, 2048], "float32"),
     "p0": ("psum", [128, 2048], "float32"), "p1": ("psum", [128, 2048], "float32"),
 }
-SEMAPHORES = (["sw", "ss", "sv", "sa", "swl", "sso", "szo", "sk", "se", "sqe", "sdn", "sqm", "sla", "slb", "ara", "arb", "loc",
-               "gov", "gos", "gav", "gas", "gbv", "gbs", "sqo", "sqa", "sqb", "sh", "sy"]
-              + ["%s%d" % (n, b) for n in ("mo", "ma", "mb", "co", "ca", "cb", "gg", "tt", "hh", "hq", "ym", "yc") for b in range(4)])
+SEMAPHORES = (["sw", "ss", "sv", "sa", "swl", "ssn", "sso", "szo", "sk", "se", "sqe", "sdn", "sx1", "sx2", "sqm", "lol", "loc",
+               "la0", "la1", "la2", "ar0", "ar1", "ar2", "arn", "gv0", "gv1", "gv2", "gs0", "gs1", "gs2", "gov", "gos",
+               "sq0", "sq1", "sq2", "sqo", "tt", "hd2", "hd3", "sh", "sy", "yc4", "ym4"]
+              + ["%s%d" % (n, b) for n in ("m0", "m1", "m2", "mn", "c0", "c1", "c2", "cn", "gg", "tp", "hh", "hq", "ym", "yc") for b in range(4)])
 
 
 def rank_program(g, core, T, topo):
@@ -39,69 +45,81 @@ def rank_program(g, core, T, topo):
     v, s, te, sy = g.vector, g.scalar, g.tensor, g.sync
     Copy = ActivationFunctionType.Copy
     cores = T.cores
-    mine = [q for q in range(N) if q // HALF == r // HALF and q != r]
-    other = [q for q in range(N) if q // HALF != r // HALF]
 
-    near = [q for q in mine if topo.chip(cores[q]) == topo.chip(core)]
-    far = [q for q in mine if q not in near]
-    off = topo.engines(core, cores[other[0]])
-    on = [e for e in topo.engines(core, cores[near[0]]) if e not in off]
+    chips = []
+    for q in range(N):
+        if chips and topo.chip(cores[chips[-1][0]]) == topo.chip(cores[q]):
+            chips[-1].append(q)
+        else:
+            chips.append([q])
+    me = [k for k in range(len(chips)) if r in chips[k]][0]
+    pos = chips[me].index(r)
+    near = chips[me][1 - pos]
+    order = sorted((1, 2, 3), key=lambda x: topo.same_plane(topo.chip(core), topo.chip(cores[chips[me ^ x][0]])))
+    far = [chips[me ^ x] for x in order]
+    off = topo.engines(core, cores[far[0][0]])
+    for x in far:
+        off = [e for e in off if e in topo.engines(core, cores[x[0]])]
+    on = [e for e in topo.engines(core, cores[near]) if e not in off]
+    W = len(off) // 2
 
     def msk(es):
         return sum(1 << e for e in es)
 
-    eng = {q: on[4 * i:4 * i + 4] for i, q in enumerate(near)}
-    w = len(off) // len(far)
-    eng.update({q: off[w * i:w * i + w] for i, q in enumerate(far)})
-    w = len(off) // len(other)
-    eng.update({q: off[w * i:w * i + w] for i, q in enumerate(other)})
-    engs = lambda src, dst: 4 if topo.chip(cores[src]) == topo.chip(cores[dst]) else len(off) // (2 if src // HALF == dst // HALF else 4)
-    place = lambda src, dst: [q for q in range(N) if q // HALF == src // HALF and q != dst].index(src)
-
-    def send(dsts, src, dst, sem):
+    def send(items, local):
         tr = []
-        for i, q in enumerate(dsts):
+        for q, es, src, dst, sem in items:
             rid, pid, _ = topo.addr(cores[q])
-            tr.append(RemoteDMATransfer(dst_ids=[DstId(rid=rid, pnc=pid)], dma_engine_mask=msk(eng[q]), remote_sem=sem,
-                                        src=src(i, q), dst=dst(place(r, q)), alu_op=0))
-        g.remote_dma_fused(tr, local_sem=S.loc)
-        return sum(len(eng[q]) for q in dsts)
-
-    inA = sum(engs(q, r) for q in mine)
-    inB = sum(engs(q, r) for q in other)
+            tr.append(RemoteDMATransfer(dst_ids=[DstId(rid=rid, pnc=pid)], dma_engine_mask=msk(es), remote_sem=sem, src=src, dst=dst, alu_op=0))
+        g.remote_dma_fused(tr, local_sem=local)
+        return sum(len(it[1]) for it in items)
 
     for k in range(8):
         (sy if k % 2 == 0 else s).dma_start(out=T.wraw[16 * k:16 * k + 16, :], in_=T.want[:]).then_inc(S.sw, 16)
     sy.dma_start(out=T.vt[:], in_=T.v[:]).then_inc(S.sv, 16)
     for k in range(8):
-        sy.dma_start(out=T.sraw[16 * k:16 * k + 16, :], in_=T.slot[:]).then_inc(S.ss, 16)
-    sy.dma_start(out=T.at[:], in_=T.a[:]).then_inc(S.sa, 16)
+        s.dma_start(out=T.sraw[16 * k:16 * k + 16, :], in_=T.slot[:]).then_inc(S.ss, 16)
 
     g.iota(T.kk[:], [[1, 128], [-1, 4]], 0, 0, allow_small_or_imprecise_dtypes=True).then_inc(S.sk, 1)
-    g.iota(T.kc[:], [[-128, 4]], 0, 4, allow_small_or_imprecise_dtypes=True).then_inc(S.sk, 1)
+    g.iota(T.kc[:], [[-128, 2]], 0, 4, allow_small_or_imprecise_dtypes=True).then_inc(S.sk, 1)
+    g.iota(T.kb[:], [[-1, 2], [-1, 4]], -256, 4, allow_small_or_imprecise_dtypes=True).then_inc(S.sk, 1)
     g.iota(T.kd[:], [[1, 128]], 0, -1, allow_small_or_imprecise_dtypes=True).then_inc(S.sk, 1)
-    gone = 0
     g.wait_ge(S.swl, 1)
-    gone += send(mine, lambda i, q: T.wl[:, L * q:L * q + L], lambda k: T.la[:, L * k:L * k + L], S.sla)
-    gone += send(other, lambda i, q: T.wl[:, L * q:L * q + L], lambda k: T.lb[:, L * k:L * k + L], S.slb)
-    for sem, dsts, qs, xs, qd, xd, arr in ((S.sqa, mine, T.qa, T.xa, T.ra, T.rxa, S.ara), (S.sqb, other, T.qb, T.xb, T.rb, T.rxb, S.arb)):
-        g.wait_ge(sem, 1)
-        gone += send(dsts, lambda i, q: qs[:, CAPP * i:CAPP * i + CAPP].bitcast(dt.uint8),
-                     lambda k: qd[:, CAPP * k:CAPP * k + CAPP].bitcast(dt.uint8), arr)
-        gone += send(dsts, lambda i, q: xs[:, CAPP * i:CAPP * i + CAPP], lambda k: xd[:, CAPP * k:CAPP * k + CAPP], arr)
+    left = 0
+    for k in range(3):
+        dst = T["l%d" % k]
+        it = [(q, off[W * i:W * i + W], T.wl[:, L * q:L * q + L], dst[:, L * pos:L * pos + L], S["la%d" % k]) for i, q in enumerate(far[k])]
+        if k == 1:
+            it.append((near, on[0:W // 2], T.wl[:, L * near:L * near + L], dst[:, 2 * L:3 * L], S.la1))
+        left += send(it, S.lol)
+    n0 = 0 if pos == 0 else 128
+    gone = 0
+    for k in range(3):
+        g.wait_ge(S["sq%d" % k], 1)
+        for what, mine, theirs, nn in (("codes", T["q%d" % k], T["r%d" % k], T.rn), ("scales", T["x%d" % k], T["rx%d" % k], T.rxn)):
+            def view(buf, a):
+                ap = buf[:, a:a + CAPP]
+                return ap.bitcast(dt.uint8) if what == "codes" else ap
+            it = [(q, off[W * i:W * i + W], view(mine, CAPP * i), view(theirs, CAPP * pos), S["ar%d" % k]) for i, q in enumerate(far[k])]
+            if k == 1:
+                it.append((near, on[0:W], view(mine, P2), view(nn, n0), S.arn))
+            gone += send(it, S.loc)
     g.wait_ge(S.loc, gone)
+    sy.wait_ge(S.lol, left)
+    sy.dma_start(out=T.at[:], in_=T.a[:]).then_inc(S.sa, 16)
 
     v.wait_ge(S.sw, 128)
     v.tensor_scalar(T.wl[:], T.wraw[:], 0.0, 4.0, AluOpType.max, AluOpType.mult).then_inc(S.swl, 1)
-    v.memset(T.town[:, 4 * CAPP:512], 0.0).then_inc(S.szo, 1)
-    v.wait_ge(S.sk, 3)
-    for b in range(4):
+    o0 = 32 if pos == 0 else 0
+    v.memset(T.town[:, 0:128] if pos == 0 else T.town[:, 384:512], 0.0).then_inc(S.szo, 1)
+    v.wait_ge(S.sk, 4)
+    for b in range(2):
         v.tensor_scalar(T.et[:, 512 * b:512 * b + 512], T.kk[:], T.kc[:, b:b + 1], None, AluOpType.is_equal).then_inc(S.se, 1)
+    for b in range(2):
+        for e in range(4):
+            v.tensor_scalar(T.et[:, 1024 + 512 * b + e:1536 + 512 * b:4], T.kk[:, e:512:4], 2.0, T.kb[:, 4 * b + e:4 * b + e + 1],
+                            AluOpType.mult, AluOpType.is_equal).then_inc(S.se, 1)
     v.tensor_scalar(T.idn[:], T.kd[:], 0.0, None, AluOpType.is_equal).then_inc(S.sdn, 1)
-    v.wait_ge(S.se, 4)
-    v.quantize_mx(T.qe[:], T.xe[:], T.et[:]).then_inc(S.sqe, 1)
-    v.wait_ge(S.ss, 128)
-    v.tensor_copy(T.so[:], T.sraw[:]).then_inc(S.sso, 1)
 
     v.wait_ge(S.sv, 16)
     s.wait_ge(S.sv, 16)
@@ -118,34 +136,61 @@ def rank_program(g, core, T, topo):
         v.wait_ge(sv_, 2)
         v.wait_ge(ss_, 2)
 
-    gather((S.sla, inA), T.ta, NA, T.la[:], S.gav, S.gas)
-    v.quantize_mx(T.qa[:], T.xa[:], T.ta[:]).then_inc(S.sqa, 1)
-    gather((S.slb, inB), T.tb, NB, T.lb[:], S.gbv, S.gbs)
-    v.quantize_mx(T.qb[:], T.xb[:], T.tb[:]).then_inc(S.sqb, 1)
-    gather((S.swl, 1), T.town, CAPP, T.wl[:, L * r:L * r + L], S.gov, S.gos)
+    for k in range(3):
+        n, came = (P2 + CAPP, 2 * W + W // 2) if k == 1 else (P2, 2 * W)
+        gather((S["la%d" % k], came), T["t%d" % k], n, T["l%d" % k][:], S["gv%d" % k], S["gs%d" % k])
+        v.quantize_mx(T["q%d" % k][:], T["x%d" % k][:], T["t%d" % k][:]).then_inc(S["sq%d" % k], 1)
+    v.wait_ge(S.se, 10)
+    v.quantize_mx(T.qe[:], T.xe[:], T.et[:]).then_inc(S.sqe, 1)
+    v.wait_ge(S.swl, 1)
+    s.wait_ge(S.swl, 1)
+    for t in range(4):
+        out, in_ = T.town[:, 4 * o0 + t:4 * (o0 + CAPP):4], T.vt[:, t:4096].indirect(T.wl[:, L * r:L * r + L])
+        if t < 2:
+            v.tensor_copy(out, in_).then_inc(S.gov, 1)
+        else:
+            s.activation(out, in_, Copy).then_inc(S.gos, 1)
+    v.wait_ge(S.gov, 2)
+    v.wait_ge(S.gos, 2)
     v.wait_ge(S.szo, 1)
-    v.quantize_mx(T.qo[:], T.xo[:], T.town[:]).then_inc(S.sqo, 1)
+    ow = 0 if pos == 0 else CAPP
+    v.quantize_mx(T.rn[:, ow:ow + 128], T.rxn[:, ow:ow + 128], T.town[:]).then_inc(S.sqo, 1)
+
+    v.wait_ge(S.ss, 128)
+    v.tensor_copy(T.sn[:], T.sraw[:]).then_inc(S.ssn, 1)
+    for u in range(2):
+        for k in range(2):
+            v.tensor_copy(T.sx[:, 32 * u + 16 * k:32 * u + 16 * k + 16], T.sraw[:, 16 * u:16 * u + 16]).then_inc(S.sx1, 1)
+    v.wait_ge(S.sx1, 4)
+    v.transpose(T.st[:], T.sx[:]).then_inc(S.sx2, 1)
+    v.wait_ge(S.sx2, 1)
+    for u in range(2):
+        for t in range(4):
+            v.tensor_copy(T.so[:, 8 * t + u:8 * t + 8:2], T.st[:, 32 * u + t:32 * u + 16:4]).then_inc(S.sso, 1)
     v.wait_ge(S.sa, 16)
     v.quantize_mx(T.qm[:], T.xm[:], T.at[:]).then_inc(S.sqm, 1)
 
     te.wait_ge(S.sqe, 1)
-    te.wait_ge(S.sqo, 1)
 
-    def unpack(ps, n, q, x, name):
+    def unpack(ps, q, x, a, name, before):
         for b in range(4):
-            if name == "mb":
-                te.wait_ge(S["co%d" % b], 1)
-            te.matmul_mx(ps[:, 512 * b:512 * b + n], T.qe[:, 128 * b:128 * b + 128], T.xe[:, 128 * b:128 * b + 128],
-                         q[:, 0:n], x[:, 0:n], True, True).then_inc(S["%s%d" % (name, b)], 1)
+            if before:
+                te.wait_ge(S["%s%d" % (before, b)], 1)
+            te.matmul_mx(ps[:, 512 * b:512 * b + P2], T.qe[:, 128 * b:128 * b + 128], T.xe[:, 128 * b:128 * b + 128],
+                         q[:, a:a + P2], x[:, a:a + P2], True, True).then_inc(S["%s%d" % (name, b)], 1)
 
-    unpack(T.p0, 128, T.qo, T.xo, "mo")
-    te.wait_ge(S.ara, 2 * inA)
-    unpack(T.p1, NA, T.ra, T.rxa, "ma")
-    te.wait_ge(S.arb, 2 * inB)
-    unpack(T.p0, NB, T.rb, T.rxb, "mb")
+    te.wait_ge(S.ar0, 4 * W)
+    unpack(T.p0, T.r0, T.rx0, 0, "m0", None)
+    te.wait_ge(S.sqo, 1)
+    te.wait_ge(S.arn, 2 * W)
+    unpack(T.p1, T.rn, T.rxn, o0, "mn", None)
+    te.wait_ge(S.ar1, 4 * W)
+    unpack(T.p0, T.r1, T.rx1, 0, "m1", "c0")
+    te.wait_ge(S.ar2, 4 * W)
+    unpack(T.p1, T.r2, T.rx2, 0, "m2", "cn")
 
-    def copy(b, out, in_, sem):
-        if b % 2 == 0:
+    def copy(qu, out, in_, sem):
+        if qu is v:
             v.tensor_copy(out, in_).then_inc(sem, 1)
         else:
             s.activation(out, in_, Copy).then_inc(sem, 1)
@@ -153,71 +198,71 @@ def rank_program(g, core, T, topo):
     def queue(b):
         return v if b % 2 == 0 else s
 
-    def runs(ranks):
-        res = []
-        for k, q in enumerate(ranks):
-            if res and res[-1][1] + res[-1][2] == q:
-                res[-1][2] += 1
-            else:
-                res.append([k, q, 1])
-        return res
+    def store(qu, k, ps, ranks, b):
+        qu.wait_ge(S["m%s%d" % (k, b)], 1)
+        a = N * CAPP * b + CAPP * ranks[0]
+        copy(qu, T.win[:, a:a + P2], ps[:, 512 * b:512 * b + P2], S["c%s%d" % (k, b)])
 
-    def store(name, m, ps, ranks, bs):
-        for b in bs:
-            queue(b).wait_ge(S["%s%d" % (m, b)], 1)
-            for k, q, n in runs(ranks):
-                copy(b, T.win[:, N * CAPP * b + CAPP * q:N * CAPP * b + CAPP * (q + n)],
-                     ps[:, 512 * b + CAPP * k:512 * b + CAPP * (k + n)], S["%s%d" % (name, b)])
-
-    store("co", "mo", T.p0, [r], range(4))
-    store("ca", "ma", T.p1, mine, range(4))
-    for pair in ((0, 1), (2, 3)):
-        store("cb", "mb", T.p0, other, pair)
-        for b in pair:
-            qu = queue(b)
-            qu.wait_ge(S.sso, 1)
-            qu.wait_ge(S["co%d" % b], 1)
-            qu.wait_ge(S["ca%d" % b], len(runs(mine)))
-            qu.wait_ge(S["cb%d" % b], 1)
-            copy(b, T.gt[:, 512 * b:512 * b + 512], T.win[:, N * CAPP * b:N * CAPP * (b + 1)].indirect(T.so[:]), S["gg%d" % b])
-
-    def turn(b):
-        te.wait_ge(S["gg%d" % b], 1)
-        for t in range(4):
-            te.transpose(T.p1[:, 512 * b + t:512 * b + 512:4], T.gt[:, 512 * b + t:512 * b + 512:4], T.idn[:]).then_inc(S["tt%d" % b], 1)
-
-    def product(b):
-        te.wait_ge(S["hq%d" % b], 1)
-        te.matmul_mx(T.p0[:, 512 * b:512 * b + 512], T.qh[:, 128 * b:128 * b + 128], T.xh[:, 128 * b:128 * b + 128],
-                     T.qm[:], T.xm[:], True, True).then_inc(S["ym%d" % b], 1)
-
-    te.wait_ge(S.sdn, 1)
-    te.wait_ge(S.sqm, 1)
-    turn(0)
-    turn(1)
-    product(0)
-    turn(2)
-    product(1)
-    turn(3)
-    product(2)
-    product(3)
+    def pick(b):
+        qu = queue(b)
+        qu.wait_ge(S.ssn if b < 2 else S.sso, 1 if b < 2 else 8)
+        for k in "0n12":
+            qu.wait_ge(S["c%s%d" % (k, b)], 1)
+        out, offs = (T.gf, T.sn) if b < 2 else (T.gb, T.so)
+        c = 512 * (b % 2)
+        copy(qu, out[:, c:c + 512], T.win[:, N * CAPP * b:N * CAPP * (b + 1)].indirect(offs[:]), S["gg%d" % b])
 
     for b in range(4):
-        c = slice(512 * b, 512 * b + 512)
-        v.wait_ge(S["tt%d" % b], 4)
-        v.tensor_copy(T.ht[:, c], T.p1[:, c]).then_inc(S["hh%d" % b], 1)
-        v.wait_ge(S["hh%d" % b], 1)
-        v.quantize_mx(T.qh[:, 128 * b:128 * b + 128], T.xh[:, 128 * b:128 * b + 128], T.ht[:, c]).then_inc(S["hq%d" % b], 1)
-        s.wait_ge(S["ym%d" % b], 1)
-        s.activation(T.yt[:, c], T.p0[:, c], Copy).then_inc(S["yc%d" % b], 1)
+        store(s, "0", T.p0, far[0], b)
+    for b in range(4):
+        store(s, "n", T.p1, chips[me], b)
+    for b in range(4):
+        store(queue(b), "1", T.p0, far[1], b)
+    for b in range(4):
+        store(queue(b), "2", T.p1, far[2], b)
+        pick(b)
 
-    for what, b in (("h", 0), ("h", 1), ("y", 0), ("h", 2), ("y", 1), ("h", 3), ("y", 2), ("y", 3)):
-        c = slice(512 * b, 512 * b + 512)
-        if what == "h":
-            sy.wait_ge(S["hh%d" % b], 1)
-            sy.dma_start(out=T.h[:, c], in_=T.ht[:, c]).then_inc(S.sh, 16)
+    te.wait_ge(S.sdn, 1)
+    for b in range(2):
+        te.wait_ge(S["gg%d" % b], 1)
+        for t in range(4):
+            te.transpose(T.p0[:, 512 * b + t:512 * b + 512:4], T.gf[:, 512 * b + t:512 * b + 512:4], T.idn[:]).then_inc(S["tp%d" % b], 1)
+        s.wait_ge(S["tp%d" % b], 4)
+        s.activation(T.ht[:, 512 * b:512 * b + 512], T.p0[:, 512 * b:512 * b + 512], Copy).then_inc(S["hh%d" % b], 1)
+    for b in (2, 3):
+        v.wait_ge(S["gg%d" % b], 1)
+        for t in range(4):
+            v.transpose(T.tr[:, 4 * (b - 2) + t:1024:8], T.gb[:, 512 * (b - 2) + 128 * t:512 * (b - 2) + 128 * t + 128]).then_inc(S.tt, 1)
+    sy.wait_ge(S.tt, 8)
+    for a in range(4):
+        sy.dma_start(out=T.ht[:, 1024 + 256 * a:1024 + 256 * a + 256], in_=T.tr[32 * a:32 * a + 32, :]).then_inc(S["hd%d" % (2 + a // 2)], 16)
+
+    def ready(qu, b):
+        if b < 2:
+            qu.wait_ge(S["hh%d" % b], 1)
         else:
-            sy.wait_ge(S["yc%d" % b], 1)
+            qu.wait_ge(S["hd%d" % b], 32)
+
+    parts = [(0, 0, 512, T.p0, 1024, s), (1, 0, 512, T.p0, 1536, s), (2, 0, 512, T.p1, 0, v), (3, 0, 256, T.p1, 512, s), (3, 256, 256, T.p1, 1024, v)]
+    for b in range(4):
+        ready(v, b)
+        v.quantize_mx(T.qh[:, 128 * b:128 * b + 128], T.xh[:, 128 * b:128 * b + 128], T.ht[:, 512 * b:512 * b + 512]).then_inc(S["hq%d" % b], 1)
+    te.wait_ge(S.sqm, 1)
+    for i, (b, a, n, ps, at, qu) in enumerate(parts):
+        te.wait_ge(S["hq%d" % b], 1)
+        te.matmul_mx(ps[:, at:at + n], T.qh[:, 128 * b:128 * b + 128], T.xh[:, 128 * b:128 * b + 128],
+                     T.qm[:, a:a + n], T.xm[:, a:a + n], True, True).then_inc(S["ym%d" % i], 1)
+        qu.wait_ge(S["ym%d" % i], 1)
+        copy(qu, T.yt[:, 512 * b + a:512 * b + a + n], ps[:, at:at + n], S["yc%d" % i])
+
+    for what, i in (("h", 0), ("h", 1), ("h", 2), ("h", 3), ("y", 0), ("y", 1), ("y", 2), ("y", 3), ("y", 4)):
+        if what == "h":
+            ready(sy, i)
+            sy.dma_start(out=T.h[:, 512 * i:512 * i + 512], in_=T.ht[:, 512 * i:512 * i + 512]).then_inc(S.sh, 16)
+        else:
+            b, a, n = parts[i][0:3]
+            c = slice(512 * b + a, 512 * b + a + n)
+            sy.wait_ge(S["yc%d" % i], 1)
             sy.dma_start(out=T.y[:, c], in_=T.yt[:, c]).then_inc(S.sy, 16)
     sy.wait_ge(S.sh, 64)
-    sy.wait_ge(S.sy, 64)
+    sy.wait_ge(S.sy, 80)

from concourse.bass import DstId, RemoteDMATransfer
from concourse.mybir import dt, AluOpType, ActivationFunctionType

N, CAPP = 8, 96
L = CAPP // 16
P2 = 2 * CAPP
E4 = "float8_e4m3fn_x4"

SCRATCH = {
    "wraw": ("sbuf", [128, N * L], "int32"), "wl": ("sbuf", [128, N * L], "uint16"),
    "sraw": ("sbuf", [128, 32], "int32"), "sn": ("sbuf", [128, 32], "uint16"), "so": ("sbuf", [128, 32], "uint16"),
    "sx": ("sbuf", [128, 64], "float32"), "st": ("sbuf", [128, 64], "float32"),
    "l0": ("sbuf", [128, 2 * L], "uint16"), "l1": ("sbuf", [128, 3 * L], "uint16"), "l2": ("sbuf", [128, 2 * L], "uint16"),
    "vt": ("sbuf", [128, 4096], "bfloat16"), "at": ("sbuf", [128, 2048], "bfloat16"),
    "t0": ("sbuf", [128, 4 * P2], "bfloat16"), "t1": ("sbuf", [128, 4 * (P2 + CAPP)], "bfloat16"), "t2": ("sbuf", [128, 4 * P2], "bfloat16"),
    "q0": ("sbuf", [128, P2], E4), "x0": ("sbuf", [128, P2], "uint8"),
    "q1": ("sbuf", [128, P2 + CAPP], E4), "x1": ("sbuf", [128, P2 + CAPP], "uint8"),
    "q2": ("sbuf", [128, P2], E4), "x2": ("sbuf", [128, P2], "uint8"),
    "town": ("sbuf", [128, 512], "bfloat16"),
    "r0": ("sbuf", [128, P2], E4), "rx0": ("sbuf", [128, P2], "uint8"),
    "r1": ("sbuf", [128, P2], E4), "rx1": ("sbuf", [128, P2], "uint8"),
    "r2": ("sbuf", [128, P2], E4), "rx2": ("sbuf", [128, P2], "uint8"),
    "rn": ("sbuf", [128, 224], E4), "rxn": ("sbuf", [128, 224], "uint8"),
    "qm": ("sbuf", [128, 512], E4), "xm": ("sbuf", [128, 512], "uint8"),
    "kk": ("sbuf", [128, 512], "bfloat16"), "kc": ("sbuf", [128, 2], "float32"), "kb": ("sbuf", [128, 8], "float32"),
    "kd": ("sbuf", [128, 128], "float32"), "idn": ("sbuf", [128, 128], "float32"),
    "et": ("sbuf", [128, 2048], "bfloat16"), "qe": ("sbuf", [128, 512], E4), "xe": ("sbuf", [128, 512], "uint8"),
    "win": ("sbuf", [128, 4 * N * CAPP], "bfloat16"),
    "gf": ("sbuf", [128, 1024], "float32"), "gb": ("sbuf", [128, 1024], "bfloat16"), "tr": ("sbuf", [128, 1024], "bfloat16"),
    "ht": ("sbuf", [128, 2048], "bfloat16"), "qh": ("sbuf", [128, 512], E4), "xh": ("sbuf", [128, 512], "uint8"),
    "yt": ("sbuf", [128, 2048], "float32"),
    "p0": ("psum", [128, 2048], "float32"), "p1": ("psum", [128, 2048], "float32"),
}
SEMAPHORES = (["sw", "ss", "sv", "sa", "swl", "ssn", "sso", "szo", "sk", "se", "sqe", "sdn", "sx1", "sx2", "sqm", "lol", "loc",
               "la0", "la1", "la2", "ar0", "ar1", "ar2", "arn", "gv0", "gv1", "gv2", "gs0", "gs1", "gs2", "gov", "gos",
               "sq0", "sq1", "sq2", "sqo", "tt", "hd2", "hd3", "sh", "sy", "yc4", "ym4"]
              + ["%s%d" % (n, b) for n in ("m0", "m1", "m2", "mn", "c0", "c1", "c2", "cn", "gg", "tp", "hh", "hq", "ym", "yc") for b in range(4)])


def rank_program(g, core, T, topo):
    r = T.rank_of(core)
    if r is None:
        return
    S = T.sem
    v, s, te, sy = g.vector, g.scalar, g.tensor, g.sync
    Copy = ActivationFunctionType.Copy
    cores = T.cores

    chips = []
    for q in range(N):
        if chips and topo.chip(cores[chips[-1][0]]) == topo.chip(cores[q]):
            chips[-1].append(q)
        else:
            chips.append([q])
    me = [k for k in range(len(chips)) if r in chips[k]][0]
    pos = chips[me].index(r)
    near = chips[me][1 - pos]
    order = sorted((1, 2, 3), key=lambda x: topo.same_plane(topo.chip(core), topo.chip(cores[chips[me ^ x][0]])))
    far = [chips[me ^ x] for x in order]
    off = topo.engines(core, cores[far[0][0]])
    for x in far:
        off = [e for e in off if e in topo.engines(core, cores[x[0]])]
    on = [e for e in topo.engines(core, cores[near]) if e not in off]
    W = len(off) // 2

    def msk(es):
        return sum(1 << e for e in es)

    def send(items, local):
        tr = []
        for q, es, src, dst, sem in items:
            rid, pid, _ = topo.addr(cores[q])
            tr.append(RemoteDMATransfer(dst_ids=[DstId(rid=rid, pnc=pid)], dma_engine_mask=msk(es), remote_sem=sem, src=src, dst=dst, alu_op=0))
        g.remote_dma_fused(tr, local_sem=local)
        return sum(len(it[1]) for it in items)

    for k in range(8):
        (sy if k % 2 == 0 else s).dma_start(out=T.wraw[16 * k:16 * k + 16, :], in_=T.want[:]).then_inc(S.sw, 16)
    sy.dma_start(out=T.vt[:], in_=T.v[:]).then_inc(S.sv, 16)
    for k in range(8):
        s.dma_start(out=T.sraw[16 * k:16 * k + 16, :], in_=T.slot[:]).then_inc(S.ss, 16)

    g.iota(T.kk[:], [[1, 128], [-1, 4]], 0, 0, allow_small_or_imprecise_dtypes=True).then_inc(S.sk, 1)
    g.iota(T.kc[:], [[-128, 2]], 0, 4, allow_small_or_imprecise_dtypes=True).then_inc(S.sk, 1)
    g.iota(T.kb[:], [[-1, 2], [-1, 4]], -256, 4, allow_small_or_imprecise_dtypes=True).then_inc(S.sk, 1)
    g.iota(T.kd[:], [[1, 128]], 0, -1, allow_small_or_imprecise_dtypes=True).then_inc(S.sk, 1)
    g.wait_ge(S.swl, 1)
    left = 0
    for k in range(3):
        dst = T["l%d" % k]
        it = [(q, off[W * i:W * i + W], T.wl[:, L * q:L * q + L], dst[:, L * pos:L * pos + L], S["la%d" % k]) for i, q in enumerate(far[k])]
        if k == 1:
            it.append((near, on[0:W // 2], T.wl[:, L * near:L * near + L], dst[:, 2 * L:3 * L], S.la1))
        left += send(it, S.lol)
    n0 = 0 if pos == 0 else 128
    gone = 0
    for k in range(3):
        g.wait_ge(S["sq%d" % k], 1)
        for what, mine, theirs, nn in (("codes", T["q%d" % k], T["r%d" % k], T.rn), ("scales", T["x%d" % k], T["rx%d" % k], T.rxn)):
            def view(buf, a):
                ap = buf[:, a:a + CAPP]
                return ap.bitcast(dt.uint8) if what == "codes" else ap
            it = [(q, off[W * i:W * i + W], view(mine, CAPP * i), view(theirs, CAPP * pos), S["ar%d" % k]) for i, q in enumerate(far[k])]
            if k == 1:
                it.append((near, on[0:W], view(mine, P2), view(nn, n0), S.arn))
            gone += send(it, S.loc)
    g.wait_ge(S.loc, gone)
    sy.wait_ge(S.lol, left)
    sy.dma_start(out=T.at[:], in_=T.a[:]).then_inc(S.sa, 16)

    v.wait_ge(S.sw, 128)
    v.tensor_scalar(T.wl[:], T.wraw[:], 0.0, 4.0, AluOpType.max, AluOpType.mult).then_inc(S.swl, 1)
    o0 = 32 if pos == 0 else 0
    v.memset(T.town[:, 0:128] if pos == 0 else T.town[:, 384:512], 0.0).then_inc(S.szo, 1)
    v.wait_ge(S.sk, 4)
    for b in range(2):
        v.tensor_scalar(T.et[:, 512 * b:512 * b + 512], T.kk[:], T.kc[:, b:b + 1], None, AluOpType.is_equal).then_inc(S.se, 1)
    for b in range(2):
        for e in range(4):
            v.tensor_scalar(T.et[:, 1024 + 512 * b + e:1536 + 512 * b:4], T.kk[:, e:512:4], 2.0, T.kb[:, 4 * b + e:4 * b + e + 1],
                            AluOpType.mult, AluOpType.is_equal).then_inc(S.se, 1)
    v.tensor_scalar(T.idn[:], T.kd[:], 0.0, None, AluOpType.is_equal).then_inc(S.sdn, 1)

    v.wait_ge(S.sv, 16)
    s.wait_ge(S.sv, 16)

    def gather(wait, tile, n, offs, sv_, ss_):
        v.wait_ge(*wait)
        s.wait_ge(*wait)
        for t in range(4):
            out, in_ = tile[:, t:4 * n:4], T.vt[:, t:4096].indirect(offs)
            if t < 2:
                v.tensor_copy(out, in_).then_inc(sv_, 1)
            else:
                s.activation(out, in_, Copy).then_inc(ss_, 1)
        v.wait_ge(sv_, 2)
        v.wait_ge(ss_, 2)

    for k in range(3):
        n, came = (P2 + CAPP, 2 * W + W // 2) if k == 1 else (P2, 2 * W)
        gather((S["la%d" % k], came), T["t%d" % k], n, T["l%d" % k][:], S["gv%d" % k], S["gs%d" % k])
        v.quantize_mx(T["q%d" % k][:], T["x%d" % k][:], T["t%d" % k][:]).then_inc(S["sq%d" % k], 1)
    v.wait_ge(S.se, 10)
    v.quantize_mx(T.qe[:], T.xe[:], T.et[:]).then_inc(S.sqe, 1)
    v.wait_ge(S.swl, 1)
    s.wait_ge(S.swl, 1)
    for t in range(4):
        out, in_ = T.town[:, 4 * o0 + t:4 * (o0 + CAPP):4], T.vt[:, t:4096].indirect(T.wl[:, L * r:L * r + L])
        if t < 2:
            v.tensor_copy(out, in_).then_inc(S.gov, 1)
        else:
            s.activation(out, in_, Copy).then_inc(S.gos, 1)
    v.wait_ge(S.gov, 2)
    v.wait_ge(S.gos, 2)
    v.wait_ge(S.szo, 1)
    ow = 0 if pos == 0 else CAPP
    v.quantize_mx(T.rn[:, ow:ow + 128], T.rxn[:, ow:ow + 128], T.town[:]).then_inc(S.sqo, 1)

    v.wait_ge(S.ss, 128)
    v.tensor_copy(T.sn[:], T.sraw[:]).then_inc(S.ssn, 1)
    for u in range(2):
        for k in range(2):
            v.tensor_copy(T.sx[:, 32 * u + 16 * k:32 * u + 16 * k + 16], T.sraw[:, 16 * u:16 * u + 16]).then_inc(S.sx1, 1)
    v.wait_ge(S.sx1, 4)
    v.transpose(T.st[:], T.sx[:]).then_inc(S.sx2, 1)
    v.wait_ge(S.sx2, 1)
    for u in range(2):
        for t in range(4):
            v.tensor_copy(T.so[:, 8 * t + u:8 * t + 8:2], T.st[:, 32 * u + t:32 * u + 16:4]).then_inc(S.sso, 1)
    v.wait_ge(S.sa, 16)
    v.quantize_mx(T.qm[:], T.xm[:], T.at[:]).then_inc(S.sqm, 1)

    te.wait_ge(S.sqe, 1)

    def unpack(ps, q, x, a, name, before):
        for b in range(4):
            if before:
                te.wait_ge(S["%s%d" % (before, b)], 1)
            te.matmul_mx(ps[:, 512 * b:512 * b + P2], T.qe[:, 128 * b:128 * b + 128], T.xe[:, 128 * b:128 * b + 128],
                         q[:, a:a + P2], x[:, a:a + P2], True, True).then_inc(S["%s%d" % (name, b)], 1)

    te.wait_ge(S.ar0, 4 * W)
    unpack(T.p0, T.r0, T.rx0, 0, "m0", None)
    te.wait_ge(S.sqo, 1)
    te.wait_ge(S.arn, 2 * W)
    unpack(T.p1, T.rn, T.rxn, o0, "mn", None)
    te.wait_ge(S.ar1, 4 * W)
    unpack(T.p0, T.r1, T.rx1, 0, "m1", "c0")
    te.wait_ge(S.ar2, 4 * W)
    unpack(T.p1, T.r2, T.rx2, 0, "m2", "cn")

    def copy(qu, out, in_, sem):
        if qu is v:
            v.tensor_copy(out, in_).then_inc(sem, 1)
        else:
            s.activation(out, in_, Copy).then_inc(sem, 1)

    def queue(b):
        return v if b % 2 == 0 else s

    def store(qu, k, ps, ranks, b):
        qu.wait_ge(S["m%s%d" % (k, b)], 1)
        a = N * CAPP * b + CAPP * ranks[0]
        copy(qu, T.win[:, a:a + P2], ps[:, 512 * b:512 * b + P2], S["c%s%d" % (k, b)])

    def pick(b):
        qu = queue(b)
        qu.wait_ge(S.ssn if b < 2 else S.sso, 1 if b < 2 else 8)
        for k in "0n12":
            qu.wait_ge(S["c%s%d" % (k, b)], 1)
        out, offs = (T.gf, T.sn) if b < 2 else (T.gb, T.so)
        c = 512 * (b % 2)
        copy(qu, out[:, c:c + 512], T.win[:, N * CAPP * b:N * CAPP * (b + 1)].indirect(offs[:]), S["gg%d" % b])

    for b in range(4):
        store(s, "0", T.p0, far[0], b)
    for b in range(4):
        store(s, "n", T.p1, chips[me], b)
    for b in range(4):
        store(queue(b), "1", T.p0, far[1], b)
    for b in range(4):
        store(queue(b), "2", T.p1, far[2], b)
        pick(b)

    te.wait_ge(S.sdn, 1)
    for b in range(2):
        te.wait_ge(S["gg%d" % b], 1)
        for t in range(4):
            te.transpose(T.p0[:, 512 * b + t:512 * b + 512:4], T.gf[:, 512 * b + t:512 * b + 512:4], T.idn[:]).then_inc(S["tp%d" % b], 1)
        s.wait_ge(S["tp%d" % b], 4)
        s.activation(T.ht[:, 512 * b:512 * b + 512], T.p0[:, 512 * b:512 * b + 512], Copy).then_inc(S["hh%d" % b], 1)
    for b in (2, 3):
        v.wait_ge(S["gg%d" % b], 1)
        for t in range(4):
            v.transpose(T.tr[:, 4 * (b - 2) + t:1024:8], T.gb[:, 512 * (b - 2) + 128 * t:512 * (b - 2) + 128 * t + 128]).then_inc(S.tt, 1)
    sy.wait_ge(S.tt, 8)
    for a in range(4):
        sy.dma_start(out=T.ht[:, 1024 + 256 * a:1024 + 256 * a + 256], in_=T.tr[32 * a:32 * a + 32, :]).then_inc(S["hd%d" % (2 + a // 2)], 16)

    def ready(qu, b):
        if b < 2:
            qu.wait_ge(S["hh%d" % b], 1)
        else:
            qu.wait_ge(S["hd%d" % b], 32)

    parts = [(0, 0, 512, T.p0, 1024, s), (1, 0, 512, T.p0, 1536, s), (2, 0, 512, T.p1, 0, v), (3, 0, 256, T.p1, 512, s), (3, 256, 256, T.p1, 1024, v)]
    for b in range(4):
        ready(v, b)
        v.quantize_mx(T.qh[:, 128 * b:128 * b + 128], T.xh[:, 128 * b:128 * b + 128], T.ht[:, 512 * b:512 * b + 512]).then_inc(S["hq%d" % b], 1)
    te.wait_ge(S.sqm, 1)
    for i, (b, a, n, ps, at, qu) in enumerate(parts):
        te.wait_ge(S["hq%d" % b], 1)
        te.matmul_mx(ps[:, at:at + n], T.qh[:, 128 * b:128 * b + 128], T.xh[:, 128 * b:128 * b + 128],
                     T.qm[:, a:a + n], T.xm[:, a:a + n], True, True).then_inc(S["ym%d" % i], 1)
        qu.wait_ge(S["ym%d" % i], 1)
        copy(qu, T.yt[:, 512 * b + a:512 * b + a + n], ps[:, at:at + n], S["yc%d" % i])

    for what, i in (("h", 0), ("h", 1), ("h", 2), ("h", 3), ("y", 0), ("y", 1), ("y", 2), ("y", 3), ("y", 4)):
        if what == "h":
            ready(sy, i)
            sy.dma_start(out=T.h[:, 512 * i:512 * i + 512], in_=T.ht[:, 512 * i:512 * i + 512]).then_inc(S.sh, 16)
        else:
            b, a, n = parts[i][0:3]
            c = slice(512 * b + a, 512 * b + a + n)
            sy.wait_ge(S["yc%d" % i], 1)
            sy.dma_start(out=T.y[:, c], in_=T.yt[:, c]).then_inc(S.sy, 16)
    sy.wait_ge(S.sh, 64)
    sy.wait_ge(S.sy, 80)
